import numpy as np
import ml_dtypes


def mxq(x, axis, fmt="e4m3"):
    dtype, down = {"e4m3": (ml_dtypes.float8_e4m3fn, 7), "e5m2": (ml_dtypes.float8_e5m2, 14)}[fmt]
    v = np.moveaxis(np.asarray(x, np.float32).astype(ml_dtypes.bfloat16).astype(np.float64), axis, -1)
    blocks = v.reshape(v.shape[:-1] + (-1, 32))
    amax = np.abs(blocks).max(-1, keepdims=True)
    byte = np.maximum(np.where(amax > 0, np.frexp(amax)[1] - 1 + 127, 0) - down, 1)
    scale = np.exp2(byte - 127.0)
    codes = (blocks / scale).astype(np.float32).astype(dtype).astype(np.float64)
    return np.moveaxis((codes * scale).reshape(v.shape), -1, axis)


WIDE = False


def mx_kscale(k):
    if not WIDE:
        return np.ones(k)
    levels = np.array([10, -10, 5, -5, 0])
    if k % 512:
        return np.exp2(np.random.permutation(np.resize(levels, k // 32))).repeat(32)
    a = np.empty((k // 512, 16))
    for p in range(k // 512):
        a[p, :8] = np.random.permutation(np.resize(levels, 8))
        for g in range(8):
            far = levels[np.abs(levels - a[p, g]) >= 10]
            a[p, g + 8] = far[np.random.randint(len(far))]
    return np.exp2(a.ravel()).repeat(32)


def f64(x):
    return np.asarray(x).astype(np.float64)


def striped(idx):
    return np.tile(idx.reshape(-1, 16).T, (8, 1)).astype(np.uint16)


def unstriped(offs):
    return offs[:16].T.reshape(-1).astype(np.int64)


E2M1 = np.array([0.0, 0.5, 1.0, 1.5, 2.0, 3.0, 4.0, 6.0, -0.0, -0.5, -1.0, -1.5, -2.0, -3.0, -4.0, -6.0])


def pack_weight(w, fmt):
    k, n = w.shape
    w = f64(np.asarray(w, np.float32).astype(ml_dtypes.bfloat16)).reshape(k // 32, 32, n)
    amax = np.abs(w).max(1)
    if fmt == "e4m3":
        byte = np.frexp(amax)[1] - 1 + 127 - 7
    else:
        mant, ex = np.frexp(amax / 6.0)
        byte = np.where(mant > 0.5, ex, ex - 1) + 127
    byte = np.clip(np.where(amax > 0, byte, 1), 1, 254)
    scaled = (w * np.exp2(127.0 - byte)[:, None, :]).reshape(k, n).astype(np.float32)
    by_word = np.ascontiguousarray(scaled.reshape(k // 512, 128, 4, n).transpose(0, 1, 3, 2))
    if fmt == "e4m3":
        words = by_word.astype(ml_dtypes.float8_e4m3fn).view(np.uint8)
    else:
        c = by_word.astype(ml_dtypes.float4_e2m1fn).view(np.uint8) & 0xF
        words = (c[..., 0::2] | (c[..., 1::2] << 4)).reshape(k // 512, 128, 2 * n)
    return np.ascontiguousarray(words), np.ascontiguousarray(byte.astype(np.uint8).reshape(k // 512, 16, n))


def unpack_weight(words, scales, fmt):
    g, _, n = scales.shape
    words = np.ascontiguousarray(words).reshape(g, 128, n, -1)
    if fmt == "e4m3":
        vals = words.view(ml_dtypes.float8_e4m3fn).astype(np.float64)
    else:
        nib = np.empty((g, 128, n, 4), np.uint8)
        nib[..., 0::2] = words & 0xF
        nib[..., 1::2] = words >> 4
        vals = E2M1[nib]
    vals = vals * np.repeat(np.exp2(scales.astype(np.float64) - 127.0), 8, axis=1)[..., None]
    return vals.transpose(0, 1, 3, 2).reshape(g * 512, n)


K, T, E, C, N = 1536, 1024, 8, 128, 512
M = 512


def by_expert(wq, xq):
    return np.concatenate([wq[e].T @ xq[:, e * C:(e + 1) * C] for e in range(E)], axis=1)


def setup_inputs():
    n = np.random.standard_normal
    s = mx_kscale(K)[:, None]
    v = mx_kscale(N)
    w = [pack_weight(m, "e2m1") for m in n((E, K, N)) / np.sqrt(K) / s[None] * v[None, None, :]]
    return {
        "xT": (n((K, T)) * s).astype(np.float32),
        "w_words": np.stack([m[0] for m in w]),
        "w_scales": np.stack([m[1] for m in w]),
        "b": (0.3 * n((N, E)) * v[:, None]).astype(np.float32),
        "wp": (n((N, M)) / np.sqrt(N) / v[:, None]).astype(np.float32),
        "gate": np.tile(np.random.uniform(0.2, 1.0, E * C), (N, 1)).astype(np.float32),
        "offs": striped(np.random.permutation(T)[:E * C]),
    }


def reference(xT, w_words, w_scales, b, wp, gate, offs):
    idx = unstriped(offs)
    w = np.stack([unpack_weight(w_words[e], w_scales[e], "e2m1") for e in range(E)])
    xq = mxq(f64(xT)[:, idx], 0, "e4m3")
    y = by_expert(w, xq)
    y = y + np.repeat(f64(b), C, axis=1)
    c = np.zeros((N, T))
    c[:, idx] = f64(gate) * y
    return mxq(f64(wp), 0, "e4m3").T @ mxq(c, 0, "e4m3")

@@ -1,0 +1,268 @@
+from contextlib import ExitStack
+
+import concourse.mybir as mybir
+from concourse.masks import make_identity
+
+F32 = mybir.dt.float32
+BF16 = mybir.dt.bfloat16
+U32 = mybir.dt.uint32
+I32 = mybir.dt.int32
+U16 = mybir.dt.uint16
+U8 = mybir.dt.uint8
+E4M3 = mybir.dt.float8_e4m3fn_x4
+E2M1 = mybir.dt.float4_e2m1fn_x4
+COPY = mybir.ActivationFunctionType.Copy
+ADD = mybir.AluOpType.add
+MULT = mybir.AluOpType.mult
+
+P = 128
+K, T, E, C, N, M = 1536, 1024, 8, 128, 512, 512
+PASSES = K // 512
+HALF = T // 2
+CHUNKS = [(0, 1), (1, 2), (2, 4), (4, 6), (6, 8)]
+FT = M // P
+
+FLOPS = 2 * T * K * N + 2 * T * N * M
+BYTES = 4 * K * T + E * PASSES * (P * 2 * N + 16 * N) + 4 * N * E + 4 * N * M + 4 * T + 2 * P * (T // 16) + 4 * M * T
+
+
+def tile_moe_nxt_lin_bias_kernel(tc, xT, w_words, w_scales, b, wp, gate, offs, out):
+    nc = tc.nc
+    with ExitStack() as ctx:
+        keep = ctx.enter_context(tc.tile_pool(name="keep", bufs=1))
+        raws = ctx.enter_context(tc.tile_pool(name="raws", bufs=6))
+        grps = ctx.enter_context(tc.tile_pool(name="grps", bufs=3))
+        work = ctx.enter_context(tc.tile_pool(name="work", bufs=3))
+        psum = ctx.enter_context(tc.psum_pool(name="psum", bufs=2))
+
+        offsets = keep.tile([P, T // 16], U16, name="offsets")
+
+        gate_rows = keep.tile([P, P], F32, name="gate_rows")
+        nc.vector.memset(gate_rows[:], 0.0)
+        b_sb = keep.tile([P, 4, E], F32, name="b_sb")
+        nc.scalar.dma_start(out=b_sb[:], in_=b.rearrange("(q r) e -> q r e", r=4))
+        nc.scalar.dma_start(out=gate_rows[0:E, :], in_=gate[0:1, :].rearrange("o (e u) -> (o e) u", u=C))
+
+        xv = xT.rearrange("(a p j) t -> a p j t", p=P, j=4)
+        x_raw = {}
+        for a in range(PASSES):
+            for h in range(2):
+                x_raw[a, h] = raws.tile([P, 4, HALF], F32, name="x_raw")
+                nc.sync.dma_start(out=x_raw[a, h][:], in_=xv[a][:, :, h * HALF:(h + 1) * HALF])
+            if a == 0:
+                nc.sync.dma_start(offsets[:], offs)
+
+        w_sc = keep.tile([P, E, PASSES, N], U8, name="w_sc", align_bytes=64)
+        nc.vector.memset(w_sc[:].rearrange("p e a n -> p (e a n)").bitcast(I32), 0)
+        x_codes, g_codes = [], []
+        for a in range(PASSES):
+            x_codes.append(keep.tile([P, T], U32, name=f"x_codes{a}", align_bytes=64))
+            g_codes.append(keep.tile([P, T], U32, name=f"g_codes{a}", align_bytes=64))
+        x_sc01 = keep.tile([P, T], U8, name="x_sc01", align_bytes=64)
+        x_sc2 = keep.tile([P, T], U8, name="x_sc2", align_bytes=64)
+        g_sc01 = keep.tile([P, T], U8, name="g_sc01", align_bytes=64)
+        g_sc1 = keep.tile([P, T], U8, name="g_sc1", align_bytes=64)
+        g_sc2 = keep.tile([P, T], U8, name="g_sc2", align_bytes=64)
+        x_scales = [x_sc01[:], x_sc01[4:P], x_sc2[:]]
+        g_scales = [g_sc01, g_sc1, g_sc2]
+
+        ident_f = keep.tile([P, P], F32, name="ident_f")
+        make_identity(nc, ident_f[:])
+        nc.gpsimd.memset(x_sc01[:], 0)
+        nc.gpsimd.memset(x_sc2[:], 0)
+        nc.gpsimd.memset(g_sc1[:], 0)
+        ident_b = keep.tile([P, P], BF16, name="ident_b")
+        make_identity(nc, ident_b[:])
+
+        def load_scales(e0, e1):
+            src = w_scales[e0:e1].rearrange("e a q n -> q (e a) n").bitcast(I32)
+            for quad in range(4):
+                dst = w_sc[32 * quad:32 * quad + 4, e0:e1].rearrange("q e a n -> q (e a) n").bitcast(I32)
+                nc.sync.dma_start(out=dst, in_=src[4 * quad:4 * quad + 4])
+
+        w_sb = []
+
+        def load_words(e):
+            w_sb.append(keep.tile([P, PASSES, 2 * N], U8, name=f"w_sb{e}", align_bytes=64))
+            nc.sync.dma_start(out=w_sb[e][:].bitcast(I32), in_=w_words[e].rearrange("a p n -> p a n").bitcast(I32))
+
+        load_scales(0, 2)
+        load_words(0)
+        load_words(1)
+        wp_raw = keep.tile([P, 4, M], F32, name="wp_raw")
+        nc.sync.dma_start(out=wp_raw[:], in_=wp.rearrange("(q r) f -> q r f", r=4))
+
+        gate_ps = psum.tile([P, 4, P], F32, name="spread")
+        nc.tensor.transpose(gate_ps[:, 0, :], gate_rows[:], ident_f[:])
+        gate_col = keep.tile([P, E], F32, name="gate_col")
+        nc.vector.tensor_copy(out=gate_col[:], in_=gate_ps[:, 0, 0:E])
+
+        gated_bias = {}
+
+        def make_gated_bias(e):
+            bank = psum.tile([P, 4, P], F32, name="spread")
+            for r in range(4):
+                nc.tensor.transpose(bank[:, r, :], b_sb[:, r, e:e + 1].to_broadcast([P, P]), ident_f[:])
+            gb = keep.tile([P, N], F32, name=f"gated_bias{e}")
+            nc.scalar.activation(gb[:], bank[:].rearrange("u r q -> u (r q)"), COPY, scale=gate_col[:, e:e + 1])
+            gated_bias[e] = gb
+
+        grouped = {}
+
+        def cast(a, h, t0, t1, engine):
+            if (a, h) not in grouped:
+                grouped[a, h] = grps.tile([P, HALF, 4], BF16, name="grouped", align_bytes=64)
+            src = x_raw[a, h][:, :, t0:t1].rearrange("p j t -> p t j")
+            if engine == "v":
+                nc.vector.tensor_copy(out=grouped[a, h][:, t0:t1, :], in_=src)
+            else:
+                nc.scalar.activation(grouped[a, h][:, t0:t1, :], src, COPY)
+
+        def quantize_tokens(a, h):
+            cols = slice(h * HALF, (h + 1) * HALF)
+            nc.vector.quantize_mx(out=x_codes[a][:, cols].bitcast(E4M3), scales=x_scales[a][:, cols], in_=grouped[a, h][:].rearrange("p t j -> p (t j)"))
+
+        def gather_words(a, s0, s1):
+            picks = offsets[:, s0 // 16:s1 // 16]
+            nc.vector.tensor_copy(out=g_codes[a][:, s0:s1], in_=x_codes[a][:].indirect(picks))
+
+        def gather_scales(dst, src, s0, s1):
+            picks = offsets[:, s0 // 16:s1 // 16]
+            nc.vector.tensor_copy(out=dst[:, s0:s1], in_=src[:].indirect(picks))
+
+        def gather_scales01(s0, s1):
+            gather_scales(g_sc01, x_sc01, s0, s1)
+            for quad in range(4):
+                nc.sync.dma_start(out=g_sc1[32 * quad:32 * quad + 4, s0:s1].bitcast(I32), in_=g_sc01[32 * quad + 4:32 * quad + 8, s0:s1].bitcast(I32))
+
+        FIRST = 2 * C
+        make_gated_bias(0)
+        make_gated_bias(1)
+        cast(0, 0, 0, HALF, "s")
+        cast(0, 1, 0, HALF, "v")
+        quantize_tokens(0, 0)
+        quantize_tokens(0, 1)
+        gather_words(0, 0, FIRST)
+        cast(1, 0, 0, HALF, "s")
+        cast(1, 1, 0, HALF, "s")
+        quantize_tokens(1, 0)
+        quantize_tokens(1, 1)
+        gather_scales01(0, FIRST)
+        gather_words(1, 0, FIRST)
+        cast(2, 0, 0, HALF, "s")
+        cast(2, 1, 0, HALF // 2, "s")
+        cast(2, 1, HALF // 2, HALF, "v")
+        quantize_tokens(2, 0)
+        quantize_tokens(2, 1)
+        gather_words(2, 0, FIRST)
+        gather_scales(g_sc2, x_sc2, 0, FIRST)
+
+        wp_codes = keep.tile([P, M], U32, name="wp_codes", align_bytes=64)
+        wp_scales = keep.tile([P, M], U8, name="wp_scales", align_bytes=64)
+        wp_grouped = keep.tile([P, M, 4], BF16, name="wp_grouped", align_bytes=64)
+
+        def quantize_wp():
+            nc.gpsimd.tensor_scalar(out=wp_grouped[:], in0=wp_raw[:].rearrange("q r f -> q f r"), scalar1=1.0, scalar2=0.0, op0=MULT, op1=ADD)
+            nc.vector.quantize_mx(out=wp_codes[:].bitcast(E4M3), scales=wp_scales[:], in_=wp_grouped[:].rearrange("q f r -> q (f r)"))
+
+        ct = {}
+        cq = {}
+        osb = {}
+        results = [keep.tile([P, T], F32, name=f"result{f}") for f in range(FT)]
+
+        def experts(c):
+            e0, e1 = CHUNKS[c]
+            ct[c] = work.tile([P, 2 * C, 4], BF16, name="ct", align_bytes=64)
+            for e in range(e0, e1):
+                slots = slice(e * C, (e + 1) * C)
+                y = psum.tile([P, N], F32, name="y")
+                for a in range(PASSES):
+                    nc.tensor.matmul_mx(
+                        out=y[:],
+                        lhsT=g_codes[a][:, slots].bitcast(E4M3),
+                        lhsT_scale=g_scales[a][:, slots],
+                        rhs=w_sb[e][:, a, :].bitcast(E2M1),
+                        rhs_scale=w_sc[:, e, a, :],
+                        start=(a == 0),
+                        stop=(a == PASSES - 1),
+                    )
+                gy = work.tile([P, 4, P], F32, name="gy")
+                nc.scalar.activation(gy[:], y[:].rearrange("u (q r) -> u r q", r=4), COPY, scale=gate_col[:, e:e + 1])
+                cs = work.tile([P, N], BF16, name="cs")
+                nc.gpsimd.tensor_tensor(out=cs[:], in0=gy[:].rearrange("u r q -> u (r q)"), in1=gated_bias[e][:], op=ADD)
+                turned = psum.tile([P, 4, P], BF16, name="turned")
+                for r in range(4):
+                    nc.tensor.transpose(turned[:, r, :], cs[:, r * P:(r + 1) * P], ident_b[:])
+                nc.scalar.copy(out=ct[c][:, (e - e0) * C:(e - e0 + 1) * C, :], in_=turned[:].rearrange("q r u -> q u r"))
+
+        def quantize_c(c):
+            n = (CHUNKS[c][1] - CHUNKS[c][0]) * C
+            codes = work.tile([P, 2 * C], U32, name="c_codes", align_bytes=64)
+            scales = work.tile([P, 2 * C], U8, name="c_scales", align_bytes=64)
+            nc.vector.quantize_mx(out=codes[:, 0:n].bitcast(E4M3), scales=scales[:, 0:n], in_=ct[c][:, 0:n, :].rearrange("q u r -> q (u r)"))
+            cq[c] = (codes, scales)
+
+        def project(c):
+            codes, scales = cq[c]
+            n = (CHUNKS[c][1] - CHUNKS[c][0]) * C
+            a_bank = 512 // n
+            osb[c] = work.tile([P, FT, n], F32, name=f"osb{n}")
+            for f0 in range(0, FT, a_bank):
+                bank = psum.tile([P, a_bank, n], F32, name="o")
+                for i in range(a_bank):
+                    f = f0 + i
+                    nc.tensor.matmul_mx(
+                        out=bank[:, i, :],
+                        lhsT=wp_codes[:, f * P:(f + 1) * P].bitcast(E4M3),
+                        lhsT_scale=wp_scales[:, f * P:(f + 1) * P],
+                        rhs=codes[:, 0:n].bitcast(E4M3),
+                        rhs_scale=scales[:, 0:n],
+                        start=True,
+                        stop=True,
+                    )
+                nc.scalar.activation(osb[c][:, f0:f0 + a_bank, :], bank[:], COPY)
+
+        def scatter(c, f):
+            e0, e1 = CHUNKS[c]
+            nc.vector.tensor_copy(out=results[f][:].indirect(offsets[:, e0 * 8:e1 * 8]), in_=osb[c][:, f, :])
+
+        experts(0)
+        load_scales(2, E)
+        for e in range(2, E):
+            load_words(e)
+        quantize_wp()
+        quantize_c(0)
+        experts(1)
+        project(0)
+        gather_words(0, FIRST, T)
+        gather_scales01(FIRST, T)
+        gather_words(1, FIRST, T)
+        quantize_c(1)
+        project(1)
+        make_gated_bias(2)
+        make_gated_bias(3)
+        gather_words(2, FIRST, 4 * C)
+        gather_scales(g_sc2, x_sc2, FIRST, 4 * C)
+        experts(2)
+        scatter(0, 0)
+        scatter(0, 1)
+        scatter(0, 2)
+        scatter(0, 3)
+        quantize_c(2)
+        project(2)
+        gather_words(2, 4 * C, T)
+        gather_scales(g_sc2, x_sc2, 4 * C, T)
+        for e in range(4, E):
+            make_gated_bias(e)
+        for c in range(1, len(CHUNKS)):
+            scatter(c, 0)
+            scatter(c, 1)
+            if 2 <= c + 1 < len(CHUNKS) and c + 1 > 2:
+                quantize_c(c + 1)
+                project(c + 1)
+            if 3 <= c + 2 < len(CHUNKS):
+                experts(c + 2)
+            scatter(c, 2)
+            scatter(c, 3)
+        for f in range(FT):
+            nc.sync.dma_start(out=out[f * P:(f + 1) * P, :], in_=results[f][:])

@@ -40,8 +40,6 @@ def tile_moe_nxt_lin_bias_kernel(tc, xT, w_words, w_scales, b, wp, gate, offs, o
         gate_rows = keep.tile([P, P], F32, name="gate_rows")
         nc.vector.memset(gate_rows[:], 0.0)
         b_sb = keep.tile([P, 4, E], F32, name="b_sb")
-        nc.scalar.dma_start(out=b_sb[:], in_=b.rearrange("(q r) e -> q r e", r=4))
-        nc.scalar.dma_start(out=gate_rows[0:E, :], in_=gate[0:1, :].rearrange("o (e u) -> (o e) u", u=C))
 
         xv = xT.rearrange("(a p j) t -> a p j t", p=P, j=4)
         x_raw = {}
@@ -49,6 +47,9 @@ def tile_moe_nxt_lin_bias_kernel(tc, xT, w_words, w_scales, b, wp, gate, offs, o
             for h in range(2):
                 x_raw[a, h] = raws.tile([P, 4, HALF], F32, name="x_raw")
                 nc.sync.dma_start(out=x_raw[a, h][:], in_=xv[a][:, :, h * HALF:(h + 1) * HALF])
+                if a == 0 and h == 0:
+                    nc.sync.dma_start(out=b_sb[:], in_=b.rearrange("(q r) e -> q r e", r=4))
+                    nc.sync.dma_start(out=gate_rows[0:E, :], in_=gate[0:1, :].rearrange("o (e u) -> (o e) u", u=C))
             if a == 0:
                 nc.sync.dma_start(offsets[:], offs)
 
@@ -71,8 +72,6 @@ def tile_moe_nxt_lin_bias_kernel(tc, xT, w_words, w_scales, b, wp, gate, offs, o
         nc.gpsimd.memset(x_sc01[:], 0)
         nc.gpsimd.memset(x_sc2[:], 0)
         nc.gpsimd.memset(g_sc1[:], 0)
-        ident_b = keep.tile([P, P], BF16, name="ident_b")
-        make_identity(nc, ident_b[:])
 
         def load_scales(e0, e1):
             src = w_scales[e0:e1].rearrange("e a q n -> q (e a) n").bitcast(I32)
@@ -138,24 +137,28 @@ def tile_moe_nxt_lin_bias_kernel(tc, xT, w_words, w_scales, b, wp, gate, offs, o
         FIRST = 2 * C
         make_gated_bias(0)
         make_gated_bias(1)
-        cast(0, 0, 0, HALF, "s")
-        cast(0, 1, 0, HALF, "v")
+        cast(0, 0, 0, HALF // 2, "s")
+        cast(0, 0, HALF // 2, HALF, "v")
+        cast(0, 1, 0, HALF // 2, "s")
+        cast(0, 1, HALF // 2, HALF, "v")
         quantize_tokens(0, 0)
         quantize_tokens(0, 1)
         gather_words(0, 0, FIRST)
         cast(1, 0, 0, HALF, "s")
-        cast(1, 1, 0, HALF, "s")
+        cast(1, 1, 0, HALF // 2, "s")
+        cast(1, 1, HALF // 2, HALF, "v")
         quantize_tokens(1, 0)
         quantize_tokens(1, 1)
         gather_scales01(0, FIRST)
         gather_words(1, 0, FIRST)
+        gather_scales01(FIRST, T)
         cast(2, 0, 0, HALF, "s")
         cast(2, 1, 0, HALF // 2, "s")
         cast(2, 1, HALF // 2, HALF, "v")
         quantize_tokens(2, 0)
         quantize_tokens(2, 1)
-        gather_words(2, 0, FIRST)
-        gather_scales(g_sc2, x_sc2, 0, FIRST)
+        gather_words(2, 0, C)
+        gather_scales(g_sc2, x_sc2, 0, C)
 
         wp_codes = keep.tile([P, M], U32, name="wp_codes", align_bytes=64)
         wp_scales = keep.tile([P, M], U8, name="wp_scales", align_bytes=64)
@@ -188,12 +191,11 @@ def tile_moe_nxt_lin_bias_kernel(tc, xT, w_words, w_scales, b, wp, gate, offs, o
                     )
                 gy = work.tile([P, 4, P], F32, name="gy")
                 nc.scalar.activation(gy[:], y[:].rearrange("u (q r) -> u r q", r=4), COPY, scale=gate_col[:, e:e + 1])
-                cs = work.tile([P, N], BF16, name="cs")
-                nc.gpsimd.tensor_tensor(out=cs[:], in0=gy[:].rearrange("u r q -> u (r q)"), in1=gated_bias[e][:], op=ADD)
-                turned = psum.tile([P, 4, P], BF16, name="turned")
+                turned = psum.tile([P, 4, P], F32, name="turned")
                 for r in range(4):
-                    nc.tensor.transpose(turned[:, r, :], cs[:, r * P:(r + 1) * P], ident_b[:])
-                nc.scalar.copy(out=ct[c][:, (e - e0) * C:(e - e0 + 1) * C, :], in_=turned[:].rearrange("q r u -> q u r"))
+                    nc.tensor.matmul(turned[:, r, :], gated_bias[e][:, r * P:(r + 1) * P], ident_f[:], start=True, stop=False, is_transpose=True)
+                    nc.tensor.matmul(turned[:, r, :], gy[:, r, :], ident_f[:], start=False, stop=True, is_transpose=True)
+                nc.scalar.activation(ct[c][:, (e - e0) * C:(e - e0 + 1) * C, :], turned[:].rearrange("q r u -> q u r"), COPY)
 
         def quantize_c(c):
             n = (CHUNKS[c][1] - CHUNKS[c][0]) * C
@@ -230,12 +232,13 @@ def tile_moe_nxt_lin_bias_kernel(tc, xT, w_words, w_scales, b, wp, gate, offs, o
         load_scales(2, E)
         for e in range(2, E):
             load_words(e)
+        gather_words(2, C, FIRST)
+        gather_scales(g_sc2, x_sc2, C, FIRST)
         quantize_wp()
         quantize_c(0)
         experts(1)
         project(0)
         gather_words(0, FIRST, T)
-        gather_scales01(FIRST, T)
         gather_words(1, FIRST, T)
         quantize_c(1)
         project(1)

@@ -21,6 +21,8 @@ PASSES = K // 512
 HALF = T // 2
 CHUNKS = [(0, 1), (1, 2), (2, 4), (4, 6), (6, 8)]
 FT = M // P
+FIRST = 2 * C
+WINDOW = 1408
 
 FLOPS = 2 * T * K * N + 2 * T * N * M
 BYTES = 4 * K * T + E * PASSES * (P * 2 * N + 16 * N) + 4 * N * E + 4 * N * M + 4 * T + 2 * P * (T // 16) + 4 * M * T
@@ -30,47 +32,55 @@ def tile_moe_nxt_lin_bias_kernel(tc, xT, w_words, w_scales, b, wp, gate, offs, o
     nc = tc.nc
     with ExitStack() as ctx:
         keep = ctx.enter_context(tc.tile_pool(name="keep", bufs=1))
-        raws = ctx.enter_context(tc.tile_pool(name="raws", bufs=6))
+        raws = ctx.enter_context(tc.tile_pool(name="raws", bufs=5))
+        biases = ctx.enter_context(tc.tile_pool(name="biases", bufs=8))
         grps = ctx.enter_context(tc.tile_pool(name="grps", bufs=3))
-        work = ctx.enter_context(tc.tile_pool(name="work", bufs=3))
+        work = ctx.enter_context(tc.tile_pool(name="work", bufs=2))
         psum = ctx.enter_context(tc.psum_pool(name="psum", bufs=2))
 
         offsets = keep.tile([P, T // 16], U16, name="offsets")
 
         gate_rows = keep.tile([P, P], F32, name="gate_rows")
-        nc.vector.memset(gate_rows[:], 0.0)
         b_sb = keep.tile([P, 4, E], F32, name="b_sb")
 
         xv = xT.rearrange("(a p j) t -> a p j t", p=P, j=4)
         x_raw = {}
-        for a in range(PASSES):
-            for h in range(2):
-                x_raw[a, h] = raws.tile([P, 4, HALF], F32, name="x_raw")
-                nc.sync.dma_start(out=x_raw[a, h][:], in_=xv[a][:, :, h * HALF:(h + 1) * HALF])
-                if a == 0 and h == 0:
-                    nc.sync.dma_start(out=b_sb[:], in_=b.rearrange("(q r) e -> q r e", r=4))
-                    nc.sync.dma_start(out=gate_rows[0:E, :], in_=gate[0:1, :].rearrange("o (e u) -> (o e) u", u=C))
-            if a == 0:
-                nc.sync.dma_start(offsets[:], offs)
+
+        def load_tokens(pool, a, t0, t1, name):
+            x_raw[a, t0] = pool.tile([P, 4, t1 - t0], F32, name=name)
+            nc.sync.dma_start(out=x_raw[a, t0][:], in_=xv[a][:, :, t0:t1])
+
+        load_tokens(raws, 0, 0, HALF, "x_raw")
+        nc.sync.dma_start(out=b_sb[:], in_=b.rearrange("(q r) e -> q r e", r=4))
+        nc.sync.dma_start(out=gate_rows[:], in_=gate[0:16, :].rearrange("n (e u) -> (n e) u", u=C))
+        load_tokens(raws, 0, HALF, 3 * HALF // 2, "x_part")
+        load_tokens(raws, 0, 3 * HALF // 2, T, "x_part")
+        nc.sync.dma_start(offsets[:], offs)
+        load_tokens(raws, 1, 0, HALF, "x_raw")
+        load_tokens(raws, 1, HALF, T, "x_raw")
+        load_tokens(raws, 2, 0, HALF, "x_raw")
+        load_tokens(raws, 2, HALF, T, "x_raw")
 
         w_sc = keep.tile([P, E, PASSES, N], U8, name="w_sc", align_bytes=64)
         nc.vector.memset(w_sc[:].rearrange("p e a n -> p (e a n)").bitcast(I32), 0)
         x_codes, g_codes = [], []
         for a in range(PASSES):
-            x_codes.append(keep.tile([P, T], U32, name=f"x_codes{a}", align_bytes=64))
+            x_codes.append(keep.tile([P, WINDOW], U32, name=f"x_codes{a}", align_bytes=64))
+            nc.vector.memset(x_codes[a][:, T:WINDOW].bitcast(I32), 0)
             g_codes.append(keep.tile([P, T], U32, name=f"g_codes{a}", align_bytes=64))
-        x_sc01 = keep.tile([P, T], U8, name="x_sc01", align_bytes=64)
-        x_sc2 = keep.tile([P, T], U8, name="x_sc2", align_bytes=64)
-        g_sc01 = keep.tile([P, T], U8, name="g_sc01", align_bytes=64)
+        x_sc0 = keep.tile([P, WINDOW], U8, name="x_sc0", align_bytes=64)
+        x_sc21 = keep.tile([P, WINDOW], U8, name="x_sc21", align_bytes=64)
+        g_sc0 = keep.tile([P, T], U8, name="g_sc0", align_bytes=64)
+        g_early = keep.tile([P, FIRST], U8, name="g_early", align_bytes=64)
+        g_sc21 = keep.tile([P, T], U8, name="g_sc21", align_bytes=64)
         g_sc1 = keep.tile([P, T], U8, name="g_sc1", align_bytes=64)
-        g_sc2 = keep.tile([P, T], U8, name="g_sc2", align_bytes=64)
-        x_scales = [x_sc01[:], x_sc01[4:P], x_sc2[:]]
-        g_scales = [g_sc01, g_sc1, g_sc2]
+        x_scales = [x_sc0[:], x_sc21[4:P], x_sc21[:]]
+        g_scales = [g_sc0, g_sc1, g_sc21]
 
         ident_f = keep.tile([P, P], F32, name="ident_f")
         make_identity(nc, ident_f[:])
-        nc.gpsimd.memset(x_sc01[:], 0)
-        nc.gpsimd.memset(x_sc2[:], 0)
+        nc.gpsimd.memset(x_sc0[:], 0)
+        nc.gpsimd.memset(x_sc21[:], 0)
         nc.gpsimd.memset(g_sc1[:], 0)
 
         def load_scales(e0, e1):
@@ -81,88 +91,100 @@ def tile_moe_nxt_lin_bias_kernel(tc, xT, w_words, w_scales, b, wp, gate, offs, o
 
         w_sb = []
 
-        def load_words(e):
-            w_sb.append(keep.tile([P, PASSES, 2 * N], U8, name=f"w_sb{e}", align_bytes=64))
-            nc.sync.dma_start(out=w_sb[e][:].bitcast(I32), in_=w_words[e].rearrange("a p n -> p a n").bitcast(I32))
+        def load_words(pool, name):
+            pair = pool.tile([P, 2, PASSES, 2 * N], U8, name=name, align_bytes=64)
+            e0 = len(w_sb)
+            nc.sync.dma_start(
+                out=pair[:].rearrange("p e a n -> p (e a) n").bitcast(I32),
+                in_=w_words[e0:e0 + 2].rearrange("e a p n -> p (e a) n").bitcast(I32),
+            )
+            w_sb.append(pair[:, 0])
+            w_sb.append(pair[:, 1])
 
-        load_scales(0, 2)
-        load_words(0)
-        load_words(1)
-        wp_raw = keep.tile([P, 4, M], F32, name="wp_raw")
-        nc.sync.dma_start(out=wp_raw[:], in_=wp.rearrange("(q r) f -> q r f", r=4))
+        load_scales(0, E)
+        load_words(keep, "w_sb")
 
         gate_ps = psum.tile([P, 4, P], F32, name="spread")
         nc.tensor.transpose(gate_ps[:, 0, :], gate_rows[:], ident_f[:])
         gate_col = keep.tile([P, E], F32, name="gate_col")
-        nc.vector.tensor_copy(out=gate_col[:], in_=gate_ps[:, 0, 0:E])
+        nc.scalar.activation(gate_col[:], gate_ps[:, 0, 0:E], COPY)
 
         gated_bias = {}
 
-        def make_gated_bias(e):
+        def make_gated_bias(e, engine="s"):
             bank = psum.tile([P, 4, P], F32, name="spread")
             for r in range(4):
                 nc.tensor.transpose(bank[:, r, :], b_sb[:, r, e:e + 1].to_broadcast([P, P]), ident_f[:])
-            gb = keep.tile([P, N], F32, name=f"gated_bias{e}")
-            nc.scalar.activation(gb[:], bank[:].rearrange("u r q -> u (r q)"), COPY, scale=gate_col[:, e:e + 1])
+            gb = biases.tile([P, N], F32, name="gated_bias")
+            if engine == "v":
+                nc.vector.tensor_scalar(out=gb[:], in0=bank[:].rearrange("u r q -> u (r q)"), scalar1=gate_col[:, e:e + 1], scalar2=None, op0=MULT)
+            else:
+                nc.scalar.activation(gb[:], bank[:].rearrange("u r q -> u (r q)"), COPY, scale=gate_col[:, e:e + 1])
             gated_bias[e] = gb
 
         grouped = {}
 
-        def cast(a, h, t0, t1, engine):
+        def cast(a, piece, t0, t1, engine):
+            h = t0 // HALF
             if (a, h) not in grouped:
                 grouped[a, h] = grps.tile([P, HALF, 4], BF16, name="grouped", align_bytes=64)
-            src = x_raw[a, h][:, :, t0:t1].rearrange("p j t -> p t j")
+            dst = grouped[a, h][:, t0 - h * HALF:t1 - h * HALF, :]
+            src = x_raw[a, piece][:, :, t0 - piece:t1 - piece].rearrange("p j t -> p t j")
             if engine == "v":
-                nc.vector.tensor_copy(out=grouped[a, h][:, t0:t1, :], in_=src)
+                nc.vector.tensor_copy(out=dst, in_=src)
             else:
-                nc.scalar.activation(grouped[a, h][:, t0:t1, :], src, COPY)
+                nc.scalar.activation(dst, src, COPY)
 
         def quantize_tokens(a, h):
             cols = slice(h * HALF, (h + 1) * HALF)
             nc.vector.quantize_mx(out=x_codes[a][:, cols].bitcast(E4M3), scales=x_scales[a][:, cols], in_=grouped[a, h][:].rearrange("p t j -> p (t j)"))
 
         def gather_words(a, s0, s1):
+            window = T if 4 * (s1 - s0) <= 3 * T else WINDOW
             picks = offsets[:, s0 // 16:s1 // 16]
-            nc.vector.tensor_copy(out=g_codes[a][:, s0:s1], in_=x_codes[a][:].indirect(picks))
+            nc.vector.tensor_copy(out=g_codes[a][:, s0:s1], in_=x_codes[a][:, 0:window].indirect(picks))
 
         def gather_scales(dst, src, s0, s1):
+            window = T if 4 * (s1 - s0) <= 3 * T else WINDOW
             picks = offsets[:, s0 // 16:s1 // 16]
-            nc.vector.tensor_copy(out=dst[:, s0:s1], in_=src[:].indirect(picks))
+            nc.vector.tensor_copy(out=dst[:, s0:s1], in_=src[:, 0:window].indirect(picks))
 
-        def gather_scales01(s0, s1):
-            gather_scales(g_sc01, x_sc01, s0, s1)
+        def move_scales(src, s0, s1):
             for quad in range(4):
-                nc.sync.dma_start(out=g_sc1[32 * quad:32 * quad + 4, s0:s1].bitcast(I32), in_=g_sc01[32 * quad + 4:32 * quad + 8, s0:s1].bitcast(I32))
+                nc.sync.dma_start(out=g_sc1[32 * quad:32 * quad + 4, s0:s1].bitcast(I32), in_=src[32 * quad + 4:32 * quad + 8, s0:s1].bitcast(I32))
 
-        FIRST = 2 * C
-        make_gated_bias(0)
-        make_gated_bias(1)
-        cast(0, 0, 0, HALF // 2, "s")
-        cast(0, 0, HALF // 2, HALF, "v")
-        cast(0, 1, 0, HALF // 2, "s")
-        cast(0, 1, HALF // 2, HALF, "v")
+        cast(0, 0, 0, 256, "s")
+        cast(0, 0, 256, 512, "v")
+        cast(0, 512, 512, 768, "s")
+        cast(0, 768, 768, 896, "s")
+        cast(0, 768, 896, 1024, "v")
         quantize_tokens(0, 0)
         quantize_tokens(0, 1)
-        gather_words(0, 0, FIRST)
-        cast(1, 0, 0, HALF, "s")
-        cast(1, 1, 0, HALF // 2, "s")
-        cast(1, 1, HALF // 2, HALF, "v")
+        make_gated_bias(0, "v")
+        make_gated_bias(1)
+        cast(1, 0, 0, 512, "s")
+        cast(1, 512, 512, 1024, "s")
         quantize_tokens(1, 0)
         quantize_tokens(1, 1)
-        gather_scales01(0, FIRST)
+        gather_scales(g_early, x_sc21, 0, FIRST)
+        move_scales(g_early, 0, FIRST)
         gather_words(1, 0, FIRST)
-        gather_scales01(FIRST, T)
-        cast(2, 0, 0, HALF, "s")
-        cast(2, 1, 0, HALF // 2, "s")
-        cast(2, 1, HALF // 2, HALF, "v")
+        gather_words(0, 0, T)
+        gather_scales(g_sc0, x_sc0, 0, T)
+        cast(2, 0, 0, 512, "s")
+        cast(2, 512, 512, 768, "s")
+        cast(2, 512, 768, 1024, "v")
         quantize_tokens(2, 0)
         quantize_tokens(2, 1)
         gather_words(2, 0, C)
-        gather_scales(g_sc2, x_sc2, 0, C)
+        gather_scales(g_sc21, x_sc21, 0, C)
+        gather_words(1, FIRST, 3 * C)
+        wp_raw = keep.tile([P, 4, M], F32, name="wp_raw")
+        nc.sync.dma_start(out=wp_raw[:], in_=wp.rearrange("(q r) f -> q r f", r=4))
 
         wp_codes = keep.tile([P, M], U32, name="wp_codes", align_bytes=64)
         wp_scales = keep.tile([P, M], U8, name="wp_scales", align_bytes=64)
-        wp_grouped = keep.tile([P, M, 4], BF16, name="wp_grouped", align_bytes=64)
+        wp_grouped = grps.tile([P, M, 4], BF16, name="grouped", align_bytes=64)
 
         def quantize_wp():
             nc.gpsimd.tensor_scalar(out=wp_grouped[:], in0=wp_raw[:].rearrange("q r f -> q f r"), scalar1=1.0, scalar2=0.0, op0=MULT, op1=ADD)
@@ -175,8 +197,10 @@ def tile_moe_nxt_lin_bias_kernel(tc, xT, w_words, w_scales, b, wp, gate, offs, o
 
         def experts(c):
             e0, e1 = CHUNKS[c]
-            ct[c] = work.tile([P, 2 * C, 4], BF16, name="ct", align_bytes=64)
+            ct[c] = work.tile([P, 4 * C, 4], BF16, name="ct", align_bytes=64)
             for e in range(e0, e1):
+                if e not in gated_bias:
+                    make_gated_bias(e)
                 slots = slice(e * C, (e + 1) * C)
                 y = psum.tile([P, N], F32, name="y")
                 for a in range(PASSES):
@@ -189,7 +213,7 @@ def tile_moe_nxt_lin_bias_kernel(tc, xT, w_words, w_scales, b, wp, gate, offs, o
                         start=(a == 0),
                         stop=(a == PASSES - 1),
                     )
-                gy = work.tile([P, 4, P], F32, name="gy")
+                gy = work.tile([P, 4, P], F32, name="gy", bufs=3)
                 nc.scalar.activation(gy[:], y[:].rearrange("u (q r) -> u r q", r=4), COPY, scale=gate_col[:, e:e + 1])
                 turned = psum.tile([P, 4, P], F32, name="turned")
                 for r in range(4):
@@ -199,8 +223,8 @@ def tile_moe_nxt_lin_bias_kernel(tc, xT, w_words, w_scales, b, wp, gate, offs, o
 
         def quantize_c(c):
             n = (CHUNKS[c][1] - CHUNKS[c][0]) * C
-            codes = work.tile([P, 2 * C], U32, name="c_codes", align_bytes=64)
-            scales = work.tile([P, 2 * C], U8, name="c_scales", align_bytes=64)
+            codes = work.tile([P, 4 * C], U32, name="c_codes", align_bytes=64)
+            scales = work.tile([P, 4 * C], U8, name="c_scales", align_bytes=64)
             nc.vector.quantize_mx(out=codes[:, 0:n].bitcast(E4M3), scales=scales[:, 0:n], in_=ct[c][:, 0:n, :].rearrange("q u r -> q (u r)"))
             cq[c] = (codes, scales)
 
@@ -229,23 +253,22 @@ def tile_moe_nxt_lin_bias_kernel(tc, xT, w_words, w_scales, b, wp, gate, offs, o
             nc.vector.tensor_copy(out=results[f][:].indirect(offsets[:, e0 * 8:e1 * 8]), in_=osb[c][:, f, :])
 
         experts(0)
-        load_scales(2, E)
-        for e in range(2, E):
-            load_words(e)
-        gather_words(2, C, FIRST)
-        gather_scales(g_sc2, x_sc2, C, FIRST)
         quantize_wp()
+        load_words(grps, "grouped")
+        load_words(grps, "grouped")
+        load_words(grps, "grouped")
         quantize_c(0)
-        experts(1)
         project(0)
-        gather_words(0, FIRST, T)
-        gather_words(1, FIRST, T)
+        gather_scales(g_sc21, x_sc21, C, T)
+        move_scales(g_sc21, FIRST, T)
+        gather_words(2, C, 3 * C)
+        experts(1)
+        gather_words(1, 3 * C, T)
         quantize_c(1)
         project(1)
-        make_gated_bias(2)
-        make_gated_bias(3)
-        gather_words(2, FIRST, 4 * C)
-        gather_scales(g_sc2, x_sc2, FIRST, 4 * C)
+        gather_words(2, 3 * C, T)
+        for e in range(2, E):
+            make_gated_bias(e)
         experts(2)
         scatter(0, 0)
         scatter(0, 1)
@@ -253,19 +276,24 @@ def tile_moe_nxt_lin_bias_kernel(tc, xT, w_words, w_scales, b, wp, gate, offs, o
         scatter(0, 3)
         quantize_c(2)
         project(2)
-        gather_words(2, 4 * C, T)
-        gather_scales(g_sc2, x_sc2, 4 * C, T)
-        for e in range(4, E):
-            make_gated_bias(e)
-        for c in range(1, len(CHUNKS)):
-            scatter(c, 0)
-            scatter(c, 1)
-            if 2 <= c + 1 < len(CHUNKS) and c + 1 > 2:
-                quantize_c(c + 1)
-                project(c + 1)
-            if 3 <= c + 2 < len(CHUNKS):
-                experts(c + 2)
-            scatter(c, 2)
-            scatter(c, 3)
+        experts(3)
+        scatter(1, 0)
+        scatter(1, 1)
+        scatter(1, 2)
+        scatter(1, 3)
+        experts(4)
+        scatter(2, 0)
+        scatter(2, 1)
+        quantize_c(3)
+        project(3)
+        scatter(2, 2)
+        scatter(2, 3)
+        scatter(3, 0)
+        scatter(3, 1)
+        quantize_c(4)
+        project(4)
+        scatter(3, 2)
+        scatter(3, 3)
         for f in range(FT):
+            scatter(4, f)
             nc.sync.dma_start(out=out[f * P:(f + 1) * P, :], in_=results[f][:])

@@ -68,20 +68,13 @@ def tile_moe_nxt_lin_bias_kernel(tc, xT, w_words, w_scales, b, wp, gate, offs, o
             x_codes.append(keep.tile([P, WINDOW], U32, name=f"x_codes{a}", align_bytes=64))
             nc.vector.memset(x_codes[a][:, T:WINDOW].bitcast(I32), 0)
             g_codes.append(keep.tile([P, T], U32, name=f"g_codes{a}", align_bytes=64))
-        x_sc0 = keep.tile([P, WINDOW], U8, name="x_sc0", align_bytes=64)
-        x_sc21 = keep.tile([P, WINDOW], U8, name="x_sc21", align_bytes=64)
-        g_sc0 = keep.tile([P, T], U8, name="g_sc0", align_bytes=64)
-        g_early = keep.tile([P, FIRST], U8, name="g_early", align_bytes=64)
-        g_sc21 = keep.tile([P, T], U8, name="g_sc21", align_bytes=64)
-        g_sc1 = keep.tile([P, T], U8, name="g_sc1", align_bytes=64)
-        x_scales = [x_sc0[:], x_sc21[4:P], x_sc21[:]]
-        g_scales = [g_sc0, g_sc1, g_sc21]
+        x_scales = [keep.tile([P, WINDOW], U8, name=f"x_scales{a}", align_bytes=64) for a in range(PASSES)]
+        g_scales = [keep.tile([P, T], U8, name=f"g_scales{a}", align_bytes=64) for a in range(PASSES)]
 
         ident_f = keep.tile([P, P], F32, name="ident_f")
         make_identity(nc, ident_f[:])
-        nc.gpsimd.memset(x_sc0[:], 0)
-        nc.gpsimd.memset(x_sc21[:], 0)
-        nc.gpsimd.memset(g_sc1[:], 0)
+        for a in range(PASSES):
+            nc.gpsimd.memset(x_scales[a][:], 0)
 
         def load_scales(e0, e1):
             src = w_scales[e0:e1].rearrange("e a q n -> q (e a) n").bitcast(I32)
@@ -101,8 +94,8 @@ def tile_moe_nxt_lin_bias_kernel(tc, xT, w_words, w_scales, b, wp, gate, offs, o
             w_sb.append(pair[:, 0])
             w_sb.append(pair[:, 1])
 
-        load_scales(0, E)
-        load_words(keep, "w_sb")
+        load_scales(0, 2)
+        load_words(keep, "w_sb01")
 
         gate_ps = psum.tile([P, 4, P], F32, name="spread")
         nc.tensor.transpose(gate_ps[:, 0, :], gate_rows[:], ident_f[:])
@@ -128,8 +121,8 @@ def tile_moe_nxt_lin_bias_kernel(tc, xT, w_words, w_scales, b, wp, gate, offs, o
             h = t0 // HALF
             if (a, h) not in grouped:
                 grouped[a, h] = grps.tile([P, HALF, 4], BF16, name="grouped", align_bytes=64)
-            dst = grouped[a, h][:, t0 - h * HALF:t1 - h * HALF, :]
-            src = x_raw[a, piece][:, :, t0 - piece:t1 - piece].rearrange("p j t -> p t j")
+            dst = grouped[a, h][:, t0 - h * HALF:t1 - h * HALF, :].rearrange("p (t i) j -> p t j i", i=4)
+            src = x_raw[a, piece][:, :, t0 - piece:t1 - piece].rearrange("p j (t i) -> p t j i", i=4)
             if engine == "v":
                 nc.vector.tensor_copy(out=dst, in_=src)
             else:
@@ -144,14 +137,10 @@ def tile_moe_nxt_lin_bias_kernel(tc, xT, w_words, w_scales, b, wp, gate, offs, o
             picks = offsets[:, s0 // 16:s1 // 16]
             nc.vector.tensor_copy(out=g_codes[a][:, s0:s1], in_=x_codes[a][:, 0:window].indirect(picks))
 
-        def gather_scales(dst, src, s0, s1):
+        def gather_scales(a, s0, s1):
             window = T if 4 * (s1 - s0) <= 3 * T else WINDOW
             picks = offsets[:, s0 // 16:s1 // 16]
-            nc.vector.tensor_copy(out=dst[:, s0:s1], in_=src[:, 0:window].indirect(picks))
-
-        def move_scales(src, s0, s1):
-            for quad in range(4):
-                nc.sync.dma_start(out=g_sc1[32 * quad:32 * quad + 4, s0:s1].bitcast(I32), in_=src[32 * quad + 4:32 * quad + 8, s0:s1].bitcast(I32))
+            nc.vector.tensor_copy(out=g_scales[a][:, s0:s1], in_=x_scales[a][:, 0:window].indirect(picks))
 
         cast(0, 0, 0, 256, "s")
         cast(0, 0, 256, 512, "v")
@@ -166,19 +155,17 @@ def tile_moe_nxt_lin_bias_kernel(tc, xT, w_words, w_scales, b, wp, gate, offs, o
         cast(1, 512, 512, 1024, "s")
         quantize_tokens(1, 0)
         quantize_tokens(1, 1)
-        gather_scales(g_early, x_sc21, 0, FIRST)
-        move_scales(g_early, 0, FIRST)
         gather_words(1, 0, FIRST)
+        gather_scales(1, 0, FIRST)
         gather_words(0, 0, T)
-        gather_scales(g_sc0, x_sc0, 0, T)
+        gather_scales(0, 0, T)
         cast(2, 0, 0, 512, "s")
         cast(2, 512, 512, 768, "s")
         cast(2, 512, 768, 1024, "v")
         quantize_tokens(2, 0)
         quantize_tokens(2, 1)
         gather_words(2, 0, C)
-        gather_scales(g_sc21, x_sc21, 0, C)
-        gather_words(1, FIRST, 3 * C)
+        gather_scales(2, 0, C)
         wp_raw = keep.tile([P, 4, M], F32, name="wp_raw")
         nc.sync.dma_start(out=wp_raw[:], in_=wp.rearrange("(q r) f -> q r f", r=4))
 
@@ -187,7 +174,7 @@ def tile_moe_nxt_lin_bias_kernel(tc, xT, w_words, w_scales, b, wp, gate, offs, o
         wp_grouped = grps.tile([P, M, 4], BF16, name="grouped", align_bytes=64)
 
         def quantize_wp():
-            nc.gpsimd.tensor_scalar(out=wp_grouped[:], in0=wp_raw[:].rearrange("q r f -> q f r"), scalar1=1.0, scalar2=0.0, op0=MULT, op1=ADD)
+            nc.gpsimd.tensor_scalar(out=wp_grouped[:].rearrange("q (f i) r -> q f r i", i=4), in0=wp_raw[:].rearrange("q r (f i) -> q f r i", i=4), scalar1=1.0, scalar2=0.0, op0=MULT, op1=ADD)
             nc.vector.quantize_mx(out=wp_codes[:].bitcast(E4M3), scales=wp_scales[:], in_=wp_grouped[:].rearrange("q f r -> q (f r)"))
 
         ct = {}
@@ -253,20 +240,23 @@ def tile_moe_nxt_lin_bias_kernel(tc, xT, w_words, w_scales, b, wp, gate, offs, o
             nc.vector.tensor_copy(out=results[f][:].indirect(offsets[:, e0 * 8:e1 * 8]), in_=osb[c][:, f, :])
 
         experts(0)
+        load_scales(2, 4)
+        load_words(keep, "w_sb23")
+        load_scales(4, E)
+        load_words(keep, "w_sb45")
+        load_words(keep, "w_sb67")
+        gather_words(2, C, FIRST)
+        gather_scales(2, C, FIRST)
+        experts(1)
+        gather_words(1, FIRST, T)
+        gather_scales(1, FIRST, T)
         quantize_wp()
-        load_words(grps, "grouped")
-        load_words(grps, "grouped")
-        load_words(grps, "grouped")
         quantize_c(0)
         project(0)
-        gather_scales(g_sc21, x_sc21, C, T)
-        move_scales(g_sc21, FIRST, T)
-        gather_words(2, C, 3 * C)
-        experts(1)
-        gather_words(1, 3 * C, T)
         quantize_c(1)
         project(1)
-        gather_words(2, 3 * C, T)
+        gather_words(2, FIRST, T)
+        gather_scales(2, FIRST, T)
         for e in range(2, E):
             make_gated_bias(e)
         experts(2)

from contextlib import ExitStack

import concourse.mybir as mybir
from concourse.masks import make_identity

F32 = mybir.dt.float32
BF16 = mybir.dt.bfloat16
U32 = mybir.dt.uint32
I32 = mybir.dt.int32
U16 = mybir.dt.uint16
U8 = mybir.dt.uint8
E4M3 = mybir.dt.float8_e4m3fn_x4
E2M1 = mybir.dt.float4_e2m1fn_x4
COPY = mybir.ActivationFunctionType.Copy
ADD = mybir.AluOpType.add
MULT = mybir.AluOpType.mult

P = 128
K, T, E, C, N, M = 1536, 1024, 8, 128, 512, 512
PASSES = K // 512
HALF = T // 2
CHUNKS = [(0, 1), (1, 2), (2, 4), (4, 6), (6, 8)]
FT = M // P
FIRST = 2 * C
WINDOW = 1408

FLOPS = 2 * T * K * N + 2 * T * N * M
BYTES = 4 * K * T + E * PASSES * (P * 2 * N + 16 * N) + 4 * N * E + 4 * N * M + 4 * T + 2 * P * (T // 16) + 4 * M * T


def tile_moe_nxt_lin_bias_kernel(tc, xT, w_words, w_scales, b, wp, gate, offs, out):
    nc = tc.nc
    with ExitStack() as ctx:
        keep = ctx.enter_context(tc.tile_pool(name="keep", bufs=1))
        raws = ctx.enter_context(tc.tile_pool(name="raws", bufs=5))
        biases = ctx.enter_context(tc.tile_pool(name="biases", bufs=8))
        grps = ctx.enter_context(tc.tile_pool(name="grps", bufs=3))
        work = ctx.enter_context(tc.tile_pool(name="work", bufs=2))
        psum = ctx.enter_context(tc.psum_pool(name="psum", bufs=2))

        offsets = keep.tile([P, T // 16], U16, name="offsets")

        gate_rows = keep.tile([P, P], F32, name="gate_rows")
        b_sb = keep.tile([P, 4, E], F32, name="b_sb")

        xv = xT.rearrange("(a p j) t -> a p j t", p=P, j=4)
        x_raw = {}

        def load_tokens(pool, a, t0, t1, name):
            x_raw[a, t0] = pool.tile([P, 4, t1 - t0], F32, name=name)
            nc.sync.dma_start(out=x_raw[a, t0][:], in_=xv[a][:, :, t0:t1])

        load_tokens(raws, 0, 0, HALF, "x_raw")
        nc.sync.dma_start(out=b_sb[:], in_=b.rearrange("(q r) e -> q r e", r=4))
        nc.sync.dma_start(out=gate_rows[:], in_=gate[0:16, :].rearrange("n (e u) -> (n e) u", u=C))
        load_tokens(raws, 0, HALF, 3 * HALF // 2, "x_part")
        load_tokens(raws, 0, 3 * HALF // 2, T, "x_part")
        nc.sync.dma_start(offsets[:], offs)
        load_tokens(raws, 1, 0, HALF, "x_raw")
        load_tokens(raws, 1, HALF, T, "x_raw")
        load_tokens(raws, 2, 0, HALF, "x_raw")
        load_tokens(raws, 2, HALF, T, "x_raw")

        w_sc = keep.tile([P, E, PASSES, N], U8, name="w_sc", align_bytes=64)
        nc.vector.memset(w_sc[:].rearrange("p e a n -> p (e a n)").bitcast(I32), 0)
        x_codes, g_codes = [], []
        for a in range(PASSES):
            x_codes.append(keep.tile([P, WINDOW], U32, name=f"x_codes{a}", align_bytes=64))
            nc.vector.memset(x_codes[a][:, T:WINDOW].bitcast(I32), 0)
            g_codes.append(keep.tile([P, T], U32, name=f"g_codes{a}", align_bytes=64))
        x_scales = [keep.tile([P, WINDOW], U8, name=f"x_scales{a}", align_bytes=64) for a in range(PASSES)]
        g_scales = [keep.tile([P, T], U8, name=f"g_scales{a}", align_bytes=64) for a in range(PASSES)]

        ident_f = keep.tile([P, P], F32, name="ident_f")
        make_identity(nc, ident_f[:])
        for a in range(PASSES):
            nc.gpsimd.memset(x_scales[a][:], 0)

        def load_scales(e0, e1):
            src = w_scales[e0:e1].rearrange("e a q n -> q (e a) n").bitcast(I32)
            for quad in range(4):
                dst = w_sc[32 * quad:32 * quad + 4, e0:e1].rearrange("q e a n -> q (e a) n").bitcast(I32)
                nc.sync.dma_start(out=dst, in_=src[4 * quad:4 * quad + 4])

        w_sb = []

        def load_words(pool, name):
            pair = pool.tile([P, 2, PASSES, 2 * N], U8, name=name, align_bytes=64)
            e0 = len(w_sb)
            nc.sync.dma_start(
                out=pair[:].rearrange("p e a n -> p (e a) n").bitcast(I32),
                in_=w_words[e0:e0 + 2].rearrange("e a p n -> p (e a) n").bitcast(I32),
            )
            w_sb.append(pair[:, 0])
            w_sb.append(pair[:, 1])

        load_scales(0, 2)
        load_words(keep, "w_sb01")

        gate_ps = psum.tile([P, 4, P], F32, name="spread")
        nc.tensor.transpose(gate_ps[:, 0, :], gate_rows[:], ident_f[:])
        gate_col = keep.tile([P, E], F32, name="gate_col")
        nc.scalar.activation(gate_col[:], gate_ps[:, 0, 0:E], COPY)

        gated_bias = {}

        def make_gated_bias(e, engine="s"):
            bank = psum.tile([P, 4, P], F32, name="spread")
            for r in range(4):
                nc.tensor.transpose(bank[:, r, :], b_sb[:, r, e:e + 1].to_broadcast([P, P]), ident_f[:])
            gb = biases.tile([P, N], F32, name="gated_bias")
            if engine == "v":
                nc.vector.tensor_scalar(out=gb[:], in0=bank[:].rearrange("u r q -> u (r q)"), scalar1=gate_col[:, e:e + 1], scalar2=None, op0=MULT)
            else:
                nc.scalar.activation(gb[:], bank[:].rearrange("u r q -> u (r q)"), COPY, scale=gate_col[:, e:e + 1])
            gated_bias[e] = gb

        grouped = {}

        def cast(a, piece, t0, t1, engine):
            h = t0 // HALF
            if (a, h) not in grouped:
                grouped[a, h] = grps.tile([P, HALF, 4], BF16, name="grouped", align_bytes=64)
            dst = grouped[a, h][:, t0 - h * HALF:t1 - h * HALF, :].rearrange("p (t i) j -> p t j i", i=4)
            src = x_raw[a, piece][:, :, t0 - piece:t1 - piece].rearrange("p j (t i) -> p t j i", i=4)
            if engine == "v":
                nc.vector.tensor_copy(out=dst, in_=src)
            else:
                nc.scalar.activation(dst, src, COPY)

        def quantize_tokens(a, h):
            cols = slice(h * HALF, (h + 1) * HALF)
            nc.vector.quantize_mx(out=x_codes[a][:, cols].bitcast(E4M3), scales=x_scales[a][:, cols], in_=grouped[a, h][:].rearrange("p t j -> p (t j)"))

        def gather_words(a, s0, s1):
            window = T if 4 * (s1 - s0) <= 3 * T else WINDOW
            picks = offsets[:, s0 // 16:s1 // 16]
            nc.vector.tensor_copy(out=g_codes[a][:, s0:s1], in_=x_codes[a][:, 0:window].indirect(picks))

        def gather_scales(a, s0, s1):
            window = T if 4 * (s1 - s0) <= 3 * T else WINDOW
            picks = offsets[:, s0 // 16:s1 // 16]
            nc.vector.tensor_copy(out=g_scales[a][:, s0:s1], in_=x_scales[a][:, 0:window].indirect(picks))

        cast(0, 0, 0, 256, "s")
        cast(0, 0, 256, 512, "v")
        cast(0, 512, 512, 768, "s")
        cast(0, 768, 768, 896, "s")
        cast(0, 768, 896, 1024, "v")
        quantize_tokens(0, 0)
        quantize_tokens(0, 1)
        make_gated_bias(0, "v")
        make_gated_bias(1)
        cast(1, 0, 0, 512, "s")
        cast(1, 512, 512, 1024, "s")
        quantize_tokens(1, 0)
        quantize_tokens(1, 1)
        gather_words(1, 0, FIRST)
        gather_scales(1, 0, FIRST)
        gather_words(0, 0, T)
        gather_scales(0, 0, T)
        cast(2, 0, 0, 512, "s")
        cast(2, 512, 512, 768, "s")
        cast(2, 512, 768, 1024, "v")
        quantize_tokens(2, 0)
        quantize_tokens(2, 1)
        gather_words(2, 0, C)
        gather_scales(2, 0, C)
        wp_raw = keep.tile([P, 4, M], F32, name="wp_raw")
        nc.sync.dma_start(out=wp_raw[:], in_=wp.rearrange("(q r) f -> q r f", r=4))

        wp_codes = keep.tile([P, M], U32, name="wp_codes", align_bytes=64)
        wp_scales = keep.tile([P, M], U8, name="wp_scales", align_bytes=64)
        wp_grouped = grps.tile([P, M, 4], BF16, name="grouped", align_bytes=64)

        def quantize_wp():
            nc.gpsimd.tensor_scalar(out=wp_grouped[:].rearrange("q (f i) r -> q f r i", i=4), in0=wp_raw[:].rearrange("q r (f i) -> q f r i", i=4), scalar1=1.0, scalar2=0.0, op0=MULT, op1=ADD)
            nc.vector.quantize_mx(out=wp_codes[:].bitcast(E4M3), scales=wp_scales[:], in_=wp_grouped[:].rearrange("q f r -> q (f r)"))

        ct = {}
        cq = {}
        osb = {}
        results = [keep.tile([P, T], F32, name=f"result{f}") for f in range(FT)]

        def experts(c):
            e0, e1 = CHUNKS[c]
            ct[c] = work.tile([P, 4 * C, 4], BF16, name="ct", align_bytes=64)
            for e in range(e0, e1):
                if e not in gated_bias:
                    make_gated_bias(e)
                slots = slice(e * C, (e + 1) * C)
                y = psum.tile([P, N], F32, name="y")
                for a in range(PASSES):
                    nc.tensor.matmul_mx(
                        out=y[:],
                        lhsT=g_codes[a][:, slots].bitcast(E4M3),
                        lhsT_scale=g_scales[a][:, slots],
                        rhs=w_sb[e][:, a, :].bitcast(E2M1),
                        rhs_scale=w_sc[:, e, a, :],
                        start=(a == 0),
                        stop=(a == PASSES - 1),
                    )
                gy = work.tile([P, 4, P], F32, name="gy", bufs=3)
                nc.scalar.activation(gy[:], y[:].rearrange("u (q r) -> u r q", r=4), COPY, scale=gate_col[:, e:e + 1])
                turned = psum.tile([P, 4, P], F32, name="turned")
                for r in range(4):
                    nc.tensor.matmul(turned[:, r, :], gated_bias[e][:, r * P:(r + 1) * P], ident_f[:], start=True, stop=False, is_transpose=True)
                    nc.tensor.matmul(turned[:, r, :], gy[:, r, :], ident_f[:], start=False, stop=True, is_transpose=True)
                nc.scalar.activation(ct[c][:, (e - e0) * C:(e - e0 + 1) * C, :], turned[:].rearrange("q r u -> q u r"), COPY)

        def quantize_c(c):
            n = (CHUNKS[c][1] - CHUNKS[c][0]) * C
            codes = work.tile([P, 4 * C], U32, name="c_codes", align_bytes=64)
            scales = work.tile([P, 4 * C], U8, name="c_scales", align_bytes=64)
            nc.vector.quantize_mx(out=codes[:, 0:n].bitcast(E4M3), scales=scales[:, 0:n], in_=ct[c][:, 0:n, :].rearrange("q u r -> q (u r)"))
            cq[c] = (codes, scales)

        def project(c):
            codes, scales = cq[c]
            n = (CHUNKS[c][1] - CHUNKS[c][0]) * C
            a_bank = 512 // n
            osb[c] = work.tile([P, FT, n], F32, name=f"osb{n}")
            for f0 in range(0, FT, a_bank):
                bank = psum.tile([P, a_bank, n], F32, name="o")
                for i in range(a_bank):
                    f = f0 + i
                    nc.tensor.matmul_mx(
                        out=bank[:, i, :],
                        lhsT=wp_codes[:, f * P:(f + 1) * P].bitcast(E4M3),
                        lhsT_scale=wp_scales[:, f * P:(f + 1) * P],
                        rhs=codes[:, 0:n].bitcast(E4M3),
                        rhs_scale=scales[:, 0:n],
                        start=True,
                        stop=True,
                    )
                nc.scalar.activation(osb[c][:, f0:f0 + a_bank, :], bank[:], COPY)

        def scatter(c, f):
            e0, e1 = CHUNKS[c]
            nc.vector.tensor_copy(out=results[f][:].indirect(offsets[:, e0 * 8:e1 * 8]), in_=osb[c][:, f, :])

        experts(0)
        load_scales(2, 4)
        load_words(keep, "w_sb23")
        load_scales(4, E)
        load_words(keep, "w_sb45")
        load_words(keep, "w_sb67")
        gather_words(2, C, FIRST)
        gather_scales(2, C, FIRST)
        experts(1)
        gather_words(1, FIRST, T)
        gather_scales(1, FIRST, T)
        quantize_wp()
        quantize_c(0)
        project(0)
        quantize_c(1)
        project(1)
        gather_words(2, FIRST, T)
        gather_scales(2, FIRST, T)
        for e in range(2, E):
            make_gated_bias(e)
        experts(2)
        scatter(0, 0)
        scatter(0, 1)
        scatter(0, 2)
        scatter(0, 3)
        quantize_c(2)
        project(2)
        experts(3)
        scatter(1, 0)
        scatter(1, 1)
        scatter(1, 2)
        scatter(1, 3)
        experts(4)
        scatter(2, 0)
        scatter(2, 1)
        quantize_c(3)
        project(3)
        scatter(2, 2)
        scatter(2, 3)
        scatter(3, 0)
        scatter(3, 1)
        quantize_c(4)
        project(4)
        scatter(3, 2)
        scatter(3, 3)
        for f in range(FT):
            scatter(4, f)
            nc.sync.dma_start(out=out[f * P:(f + 1) * P, :], in_=results[f][:])
